import numpy as np
import ml_dtypes


def mxq(x, axis, fmt="e4m3"):
    dtype, down = {"e4m3": (ml_dtypes.float8_e4m3fn, 7), "e5m2": (ml_dtypes.float8_e5m2, 14)}[fmt]
    v = np.moveaxis(np.asarray(x, np.float32).astype(ml_dtypes.bfloat16).astype(np.float64), axis, -1)
    blocks = v.reshape(v.shape[:-1] + (-1, 32))
    amax = np.abs(blocks).max(-1, keepdims=True)
    byte = np.maximum(np.where(amax > 0, np.frexp(amax)[1] - 1 + 127, 0) - down, 1)
    scale = np.exp2(byte - 127.0)
    codes = (blocks / scale).astype(np.float32).astype(dtype).astype(np.float64)
    return np.moveaxis((codes * scale).reshape(v.shape), -1, axis)


WIDE = False


def mx_kscale(k):
    if not WIDE:
        return np.ones(k)
    levels = np.array([10, -10, 5, -5, 0])
    if k % 512:
        return np.exp2(np.random.permutation(np.resize(levels, k // 32))).repeat(32)
    a = np.empty((k // 512, 16))
    for p in range(k // 512):
        a[p, :8] = np.random.permutation(np.resize(levels, 8))
        for g in range(8):
            far = levels[np.abs(levels - a[p, g]) >= 10]
            a[p, g + 8] = far[np.random.randint(len(far))]
    return np.exp2(a.ravel()).repeat(32)


def f64(x):
    return np.asarray(x).astype(np.float64)


def striped(idx):
    return np.tile(idx.reshape(-1, 16).T, (8, 1)).astype(np.uint16)


def unstriped(offs):
    return offs[:16].T.reshape(-1).astype(np.int64)


def gelu(v):
    return 0.5 * v * (1.0 + np.tanh(np.sqrt(2.0 / np.pi) * (v + 0.044715 * v**3)))


K, T, S, N = 1536, 1024, 512, 128


def setup_inputs():
    n = np.random.standard_normal
    s = mx_kscale(K)[:, None]
    return {
        "xT": (n((K, S)) * s).astype(np.float32),
        "w": (n((K, N)) / np.sqrt(K) / s).astype(np.float32),
        "b": (0.3 * n((N, 1))).astype(np.float32),
        "gate": np.tile(np.random.uniform(0.2, 1.0, S), (N, 1)).astype(np.float32),
        "offs": striped(np.random.permutation(T)[:S]),
    }


def reference(xT, w, b, gate, offs):
    idx = unstriped(offs)
    xq = mxq(f64(xT), 0, "e4m3")
    y = mxq(f64(w), 0, "e4m3").T @ xq
    y = gelu(y + f64(b))
    out = np.zeros((N, T))
    out[:, idx] = f64(gate) * y
    return out

@@ -1,0 +1,132 @@
+from contextlib import ExitStack
+
+import concourse.mybir as mybir
+
+K, T, S, N = 1536, 1024, 512, 128
+FLOPS = 2 * K * S * N
+
+F32 = mybir.dt.float32
+BF16 = mybir.dt.bfloat16
+U32 = mybir.dt.uint32
+U16 = mybir.dt.uint16
+U8 = mybir.dt.uint8
+FP8X4 = mybir.dt.float8_e4m3fn_x4
+GELU = mybir.ActivationFunctionType.Gelu_apprx_tanh
+
+P = 128
+PACK = 4
+K_PASS = P * PACK
+PASSES = K // K_PASS
+CHUNK = 128
+CHUNKS = S // CHUNK
+LANES = 16
+RUN = 4
+
+
+def tile_picked_place_lin_gelu_sub_l_kernel(tc, xT, w, b, gate, offs, out):
+    nc = tc.nc
+    last = PASSES - 1
+
+    with ExitStack() as ctx:
+        keep = ctx.enter_context(tc.tile_pool(name="keep", bufs=1))
+        psum = ctx.enter_context(tc.psum_pool(name="psum", bufs=1))
+
+        offsets = keep.tile([P, S // LANES], U16, name="offsets")
+        bias = keep.tile([P, 1], F32, name="bias")
+        window = keep.tile([P, T], F32, name="window")
+        warm_in = keep.tile([P, 1], F32, name="warm_in")
+        warm_out = keep.tile([P, 1], F32, name="warm_out")
+
+        def load_rows(name, rows):
+            raw = keep.tile([P, PACK, rows.shape[1]], F32, name=name)
+            nc.sync.dma_start(out=raw[:], in_=rows.rearrange("(p j) c -> p j c", j=PACK))
+            return raw
+
+        def interleave(copy, name, raw):
+            width = raw.shape[2]
+            grouped = keep.tile([P, width * PACK], BF16, name=name, align_bytes=64)
+            copy(
+                out=grouped[:].rearrange("p (c i j) -> p c j i", i=RUN, j=PACK),
+                in_=raw.rearrange("p j (c i) -> p c j i", i=RUN),
+            )
+            return grouped
+
+        def quantize(name, grouped):
+            width = grouped.shape[1] // PACK
+            codes = keep.tile([P, width], U32, name=name + "_codes", align_bytes=64)
+            scales = keep.tile([P, width], U8, name=name + "_scales", align_bytes=64)
+            nc.vector.quantize_mx(out=codes[:].bitcast(FP8X4), scales=scales[:], in_=grouped[:])
+            return codes, scales
+
+        def k_rows(c):
+            return slice(c * K_PASS, (c + 1) * K_PASS)
+
+        def cols(i, n=1):
+            return slice(i * CHUNK, (i + n) * CHUNK)
+
+        nc.scalar.dma_start(out=bias[:], in_=b)
+        nc.vector.memset(warm_in[:], 0.0)
+        nc.scalar.activation(out=warm_out[:], in_=warm_in[:], func=GELU)
+        nc.vector.memset(window[:], 0.0)
+
+        x_raw = [load_rows("x_raw%d" % c, xT[k_rows(c), :]) for c in range(last)]
+        nc.sync.dma_start(offsets[:], offs)
+        w_raw = [load_rows("w_raw%d" % c, w[k_rows(c), :]) for c in range(PASSES)]
+        gates = [keep.tile([P, 2 * CHUNK], F32, name="gate%d" % h) for h in range(2)]
+        tail_raw = []
+        for i in range(CHUNKS):
+            tail_raw.append(load_rows("x_tail%d" % i, xT[k_rows(last), cols(i)]))
+            if i == 0:
+                nc.sync.dma_start(out=gates[0][:], in_=gate[:, cols(0, 2)])
+            if i == CHUNKS - 1:
+                nc.sync.dma_start(out=gates[1][:], in_=gate[:, cols(2, 2)])
+
+        x_mx = {}
+        for c in range(last):
+            left = interleave(nc.vector.tensor_copy, "x_left%d" % c, x_raw[c][:, :, cols(0, 2)])
+            right = interleave(nc.scalar.copy, "x_right%d" % c, x_raw[c][:, :, cols(2, 2)])
+            x_mx[c, 0] = quantize("x_left%d" % c, left)
+            x_mx[c, 1] = quantize("x_right%d" % c, right)
+
+        w_copy = [nc.vector.tensor_copy, nc.scalar.copy, nc.vector.tensor_copy]
+        w_mx = []
+        for c in range(PASSES):
+            w_mx.append(quantize("w%d" % c, interleave(w_copy[c], "w_grouped%d" % c, w_raw[c][:])))
+
+        acc = [psum.tile([N, CHUNK], F32, name="acc%d" % i) for i in range(CHUNKS)]
+
+        def multiply(c, i, codes, scales):
+            nc.tensor.matmul_mx(
+                out=acc[i][:],
+                lhsT=w_mx[c][0][:].bitcast(FP8X4),
+                lhsT_scale=w_mx[c][1][:],
+                rhs=codes.bitcast(FP8X4),
+                rhs_scale=scales,
+                start=(c == 0),
+                stop=(c == last),
+            )
+
+        for c in range(last):
+            for i in range(CHUNKS):
+                codes, scales = x_mx[c, i // 2]
+                multiply(c, i, codes[:, cols(i % 2)], scales[:, cols(i % 2)])
+
+        def finish(i):
+            y = keep.tile([N, CHUNK], F32, name="y%d" % i)
+            nc.scalar.activation(out=y[:], in_=acc[i][:], func=GELU, bias=bias[:])
+            per = CHUNK // LANES
+            nc.vector.tensor_tensor(
+                window[:].indirect(offsets[:, i * per : (i + 1) * per]),
+                y[:],
+                gates[i // 2][:, cols(i % 2)],
+                mybir.AluOpType.mult,
+            )
+
+        for i in range(CHUNKS):
+            codes, scales = quantize("x_tail%d" % i, interleave(nc.scalar.copy, "x_tailg%d" % i, tail_raw[i][:]))
+            multiply(last, i, codes[:], scales[:])
+            if i > 0:
+                finish(i - 1)
+        finish(CHUNKS - 1)
+
+        nc.sync.dma_start(out=out, in_=window[:])

@@ -37,96 +37,108 @@ def tile_picked_place_lin_gelu_sub_l_kernel(tc, xT, w, b, gate, offs, out):
         warm_in = keep.tile([P, 1], F32, name="warm_in")
         warm_out = keep.tile([P, 1], F32, name="warm_out")
 
-        def load_rows(name, rows):
-            raw = keep.tile([P, PACK, rows.shape[1]], F32, name=name)
-            nc.sync.dma_start(out=raw[:], in_=rows.rearrange("(p j) c -> p j c", j=PACK))
-            return raw
-
-        def interleave(copy, name, raw):
-            width = raw.shape[2]
-            grouped = keep.tile([P, width * PACK], BF16, name=name, align_bytes=64)
-            copy(
-                out=grouped[:].rearrange("p (c i j) -> p c j i", i=RUN, j=PACK),
-                in_=raw.rearrange("p j (c i) -> p c j i", i=RUN),
-            )
-            return grouped
-
-        def quantize(name, grouped):
-            width = grouped.shape[1] // PACK
-            codes = keep.tile([P, width], U32, name=name + "_codes", align_bytes=64)
-            scales = keep.tile([P, width], U8, name=name + "_scales", align_bytes=64)
-            nc.vector.quantize_mx(out=codes[:].bitcast(FP8X4), scales=scales[:], in_=grouped[:])
-            return codes, scales
-
-        def k_rows(c):
-            return slice(c * K_PASS, (c + 1) * K_PASS)
-
-        def cols(i, n=1):
-            return slice(i * CHUNK, (i + n) * CHUNK)
-
         nc.scalar.dma_start(out=bias[:], in_=b)
         nc.vector.memset(warm_in[:], 0.0)
         nc.scalar.activation(out=warm_out[:], in_=warm_in[:], func=GELU)
         nc.vector.memset(window[:], 0.0)
-
-        x_raw = [load_rows("x_raw%d" % c, xT[k_rows(c), :]) for c in range(last)]
+        gates = keep.tile([P, S], F32, name="gates")
+        r_w012 = keep.tile([P, 3, PACK, N], F32, name="r_w012")
+        nc.sync.dma_start(out=r_w012[:], in_=w[0:1536, :].rearrange("(c p j) n -> p c j n", p=P, j=PACK))
+        g_w012 = keep.tile([P, 1536], BF16, name="g_w012", align_bytes=64)
+        c_w012 = keep.tile([P, 384], U32, name="c_w012", align_bytes=64)
+        s_w012 = keep.tile([P, 384], U8, name="s_w012", align_bytes=64)
+        r_x0AB = keep.tile([P, PACK, 256], F32, name="r_x0AB")
+        nc.sync.dma_start(out=r_x0AB[:], in_=xT[0:512, 0:256].rearrange("(p j) n -> p j n", j=PACK))
+        g_x0AB = keep.tile([P, 1024], BF16, name="g_x0AB", align_bytes=64)
+        c_x0AB = keep.tile([P, 256], U32, name="c_x0AB", align_bytes=64)
+        s_x0AB = keep.tile([P, 256], U8, name="s_x0AB", align_bytes=64)
+        r_x1AB = keep.tile([P, PACK, 256], F32, name="r_x1AB")
+        nc.sync.dma_start(out=r_x1AB[:], in_=xT[512:1024, 0:256].rearrange("(p j) n -> p j n", j=PACK))
+        g_x1AB = keep.tile([P, 1024], BF16, name="g_x1AB", align_bytes=64)
+        c_x1AB = keep.tile([P, 256], U32, name="c_x1AB", align_bytes=64)
+        s_x1AB = keep.tile([P, 256], U8, name="s_x1AB", align_bytes=64)
+        r_x2AB = keep.tile([P, PACK, 256], F32, name="r_x2AB")
+        nc.sync.dma_start(out=r_x2AB[:], in_=xT[1024:1536, 0:256].rearrange("(p j) n -> p j n", j=PACK))
+        g_x2AB = keep.tile([P, 1024], BF16, name="g_x2AB", align_bytes=64)
+        c_x2AB = keep.tile([P, 256], U32, name="c_x2AB", align_bytes=64)
+        s_x2AB = keep.tile([P, 256], U8, name="s_x2AB", align_bytes=64)
+        r_x0CD = keep.tile([P, PACK, 256], F32, name="r_x0CD")
+        nc.sync.dma_start(out=r_x0CD[:], in_=xT[0:512, 256:512].rearrange("(p j) n -> p j n", j=PACK))
+        g_x0CD = keep.tile([P, 1024], BF16, name="g_x0CD", align_bytes=64)
+        c_x0CD = keep.tile([P, 256], U32, name="c_x0CD", align_bytes=64)
+        s_x0CD = keep.tile([P, 256], U8, name="s_x0CD", align_bytes=64)
         nc.sync.dma_start(offsets[:], offs)
-        w_raw = [load_rows("w_raw%d" % c, w[k_rows(c), :]) for c in range(PASSES)]
-        gates = [keep.tile([P, 2 * CHUNK], F32, name="gate%d" % h) for h in range(2)]
-        tail_raw = []
-        for i in range(CHUNKS):
-            tail_raw.append(load_rows("x_tail%d" % i, xT[k_rows(last), cols(i)]))
-            if i == 0:
-                nc.sync.dma_start(out=gates[0][:], in_=gate[:, cols(0, 2)])
-            if i == CHUNKS - 1:
-                nc.sync.dma_start(out=gates[1][:], in_=gate[:, cols(2, 2)])
-
-        x_mx = {}
-        for c in range(last):
-            left = interleave(nc.vector.tensor_copy, "x_left%d" % c, x_raw[c][:, :, cols(0, 2)])
-            right = interleave(nc.scalar.copy, "x_right%d" % c, x_raw[c][:, :, cols(2, 2)])
-            x_mx[c, 0] = quantize("x_left%d" % c, left)
-            x_mx[c, 1] = quantize("x_right%d" % c, right)
-
-        w_copy = [nc.vector.tensor_copy, nc.scalar.copy, nc.vector.tensor_copy]
-        w_mx = []
-        for c in range(PASSES):
-            w_mx.append(quantize("w%d" % c, interleave(w_copy[c], "w_grouped%d" % c, w_raw[c][:])))
-
+        r_x1C = keep.tile([P, PACK, 128], F32, name="r_x1C")
+        nc.sync.dma_start(out=r_x1C[:], in_=xT[512:1024, 256:384].rearrange("(p j) n -> p j n", j=PACK))
+        g_x1C = keep.tile([P, 512], BF16, name="g_x1C", align_bytes=64)
+        c_x1C = keep.tile([P, 128], U32, name="c_x1C", align_bytes=64)
+        s_x1C = keep.tile([P, 128], U8, name="s_x1C", align_bytes=64)
+        nc.sync.dma_start(out=gates[:, 0:256], in_=gate[:, 0:256])
+        r_x2C = keep.tile([P, PACK, 128], F32, name="r_x2C")
+        nc.sync.dma_start(out=r_x2C[:], in_=xT[1024:1536, 256:384].rearrange("(p j) n -> p j n", j=PACK))
+        g_x2C = keep.tile([P, 512], BF16, name="g_x2C", align_bytes=64)
+        c_x2C = keep.tile([P, 128], U32, name="c_x2C", align_bytes=64)
+        s_x2C = keep.tile([P, 128], U8, name="s_x2C", align_bytes=64)
+        r_x1D = keep.tile([P, PACK, 128], F32, name="r_x1D")
+        nc.sync.dma_start(out=r_x1D[:], in_=xT[512:1024, 384:512].rearrange("(p j) n -> p j n", j=PACK))
+        g_x1D = keep.tile([P, 512], BF16, name="g_x1D", align_bytes=64)
+        c_x1D = keep.tile([P, 128], U32, name="c_x1D", align_bytes=64)
+        s_x1D = keep.tile([P, 128], U8, name="s_x1D", align_bytes=64)
+        r_x2D = keep.tile([P, PACK, 128], F32, name="r_x2D")
+        nc.sync.dma_start(out=r_x2D[:], in_=xT[1024:1536, 384:512].rearrange("(p j) n -> p j n", j=PACK))
+        g_x2D = keep.tile([P, 512], BF16, name="g_x2D", align_bytes=64)
+        c_x2D = keep.tile([P, 128], U32, name="c_x2D", align_bytes=64)
+        s_x2D = keep.tile([P, 128], U8, name="s_x2D", align_bytes=64)
+        nc.sync.dma_start(out=gates[:, 256:512], in_=gate[:, 256:512])
         acc = [psum.tile([N, CHUNK], F32, name="acc%d" % i) for i in range(CHUNKS)]
-
-        def multiply(c, i, codes, scales):
-            nc.tensor.matmul_mx(
-                out=acc[i][:],
-                lhsT=w_mx[c][0][:].bitcast(FP8X4),
-                lhsT_scale=w_mx[c][1][:],
-                rhs=codes.bitcast(FP8X4),
-                rhs_scale=scales,
-                start=(c == 0),
-                stop=(c == last),
-            )
-
-        for c in range(last):
-            for i in range(CHUNKS):
-                codes, scales = x_mx[c, i // 2]
-                multiply(c, i, codes[:, cols(i % 2)], scales[:, cols(i % 2)])
-
-        def finish(i):
-            y = keep.tile([N, CHUNK], F32, name="y%d" % i)
-            nc.scalar.activation(out=y[:], in_=acc[i][:], func=GELU, bias=bias[:])
-            per = CHUNK // LANES
-            nc.vector.tensor_tensor(
-                window[:].indirect(offsets[:, i * per : (i + 1) * per]),
-                y[:],
-                gates[i // 2][:, cols(i % 2)],
-                mybir.AluOpType.mult,
-            )
-
-        for i in range(CHUNKS):
-            codes, scales = quantize("x_tail%d" % i, interleave(nc.scalar.copy, "x_tailg%d" % i, tail_raw[i][:]))
-            multiply(last, i, codes[:], scales[:])
-            if i > 0:
-                finish(i - 1)
-        finish(CHUNKS - 1)
-
+        y = keep.tile([N, S], F32, name="y")
+        nc.vector.tensor_copy(out=g_w012[:, 0:512].rearrange("p (c i j) -> p c j i", i=RUN, j=PACK), in_=r_w012[:, 0, :, 0:128].rearrange("p j (c i) -> p c j i", i=RUN))
+        nc.vector.tensor_copy(out=g_w012[:, 512:1024].rearrange("p (c i j) -> p c j i", i=RUN, j=PACK), in_=r_w012[:, 1, :, 0:128].rearrange("p j (c i) -> p c j i", i=RUN))
+        nc.scalar.copy(out=g_x0AB[:, 512:1024].rearrange("p (c i j) -> p c j i", i=RUN, j=PACK), in_=r_x0AB[:, :, 128:256].rearrange("p j (c i) -> p c j i", i=RUN))
+        nc.vector.tensor_copy(out=g_x0AB[:, 0:512].rearrange("p (c i j) -> p c j i", i=RUN, j=PACK), in_=r_x0AB[:, :, 0:128].rearrange("p j (c i) -> p c j i", i=RUN))
+        nc.vector.quantize_mx(out=c_x0AB[:, 0:128].bitcast(FP8X4), scales=s_x0AB[:, 0:128], in_=g_x0AB[:, 0:512])
+        nc.vector.quantize_mx(out=c_w012[:, 0:128].bitcast(FP8X4), scales=s_w012[:, 0:128], in_=g_w012[:, 0:512])
+        nc.tensor.matmul_mx(out=acc[0][:], lhsT=c_w012[:, 0:128].bitcast(FP8X4), lhsT_scale=s_w012[:, 0:128], rhs=c_x0AB[:, 0:128].bitcast(FP8X4), rhs_scale=s_x0AB[:, 0:128], start=True, stop=False)
+        nc.vector.tensor_copy(out=g_x1AB[:, 512:1024].rearrange("p (c i j) -> p c j i", i=RUN, j=PACK), in_=r_x1AB[:, :, 128:256].rearrange("p j (c i) -> p c j i", i=RUN))
+        nc.vector.quantize_mx(out=c_x1AB[:, 128:256].bitcast(FP8X4), scales=s_x1AB[:, 128:256], in_=g_x1AB[:, 512:1024])
+        nc.scalar.copy(out=g_x2AB[:, 768:1024].rearrange("p (c i j) -> p c j i", i=RUN, j=PACK), in_=r_x2AB[:, :, 192:256].rearrange("p j (c i) -> p c j i", i=RUN))
+        nc.vector.tensor_copy(out=g_x2AB[:, 512:768].rearrange("p (c i j) -> p c j i", i=RUN, j=PACK), in_=r_x2AB[:, :, 128:192].rearrange("p j (c i) -> p c j i", i=RUN))
+        nc.vector.quantize_mx(out=c_x0AB[:, 128:256].bitcast(FP8X4), scales=s_x0AB[:, 128:256], in_=g_x0AB[:, 512:1024])
+        nc.tensor.matmul_mx(out=acc[1][:], lhsT=c_w012[:, 0:128].bitcast(FP8X4), lhsT_scale=s_w012[:, 0:128], rhs=c_x0AB[:, 128:256].bitcast(FP8X4), rhs_scale=s_x0AB[:, 128:256], start=True, stop=False)
+        nc.scalar.copy(out=g_w012[:, 1024:1536].rearrange("p (c i j) -> p c j i", i=RUN, j=PACK), in_=r_w012[:, 2, :, 0:128].rearrange("p j (c i) -> p c j i", i=RUN))
+        nc.vector.quantize_mx(out=c_w012[:, 128:384].bitcast(FP8X4), scales=s_w012[:, 128:384], in_=g_w012[:, 512:1536])
+        nc.tensor.matmul_mx(out=acc[1][:], lhsT=c_w012[:, 128:256].bitcast(FP8X4), lhsT_scale=s_w012[:, 128:256], rhs=c_x1AB[:, 128:256].bitcast(FP8X4), rhs_scale=s_x1AB[:, 128:256], start=False, stop=False)
+        nc.scalar.copy(out=g_x1AB[:, 0:512].rearrange("p (c i j) -> p c j i", i=RUN, j=PACK), in_=r_x1AB[:, :, 0:128].rearrange("p j (c i) -> p c j i", i=RUN))
+        nc.vector.quantize_mx(out=c_x1AB[:, 0:128].bitcast(FP8X4), scales=s_x1AB[:, 0:128], in_=g_x1AB[:, 0:512])
+        nc.tensor.matmul_mx(out=acc[0][:], lhsT=c_w012[:, 128:256].bitcast(FP8X4), lhsT_scale=s_w012[:, 128:256], rhs=c_x1AB[:, 0:128].bitcast(FP8X4), rhs_scale=s_x1AB[:, 0:128], start=False, stop=False)
+        nc.vector.tensor_copy(out=g_x2AB[:, 0:512].rearrange("p (c i j) -> p c j i", i=RUN, j=PACK), in_=r_x2AB[:, :, 0:128].rearrange("p j (c i) -> p c j i", i=RUN))
+        nc.vector.tensor_copy(out=g_x0CD[:, 512:1024].rearrange("p (c i j) -> p c j i", i=RUN, j=PACK), in_=r_x0CD[:, :, 128:256].rearrange("p j (c i) -> p c j i", i=RUN))
+        nc.vector.quantize_mx(out=c_x0CD[:, 128:256].bitcast(FP8X4), scales=s_x0CD[:, 128:256], in_=g_x0CD[:, 512:1024])
+        nc.tensor.matmul_mx(out=acc[3][:], lhsT=c_w012[:, 0:128].bitcast(FP8X4), lhsT_scale=s_w012[:, 0:128], rhs=c_x0CD[:, 128:256].bitcast(FP8X4), rhs_scale=s_x0CD[:, 128:256], start=True, stop=False)
+        nc.vector.quantize_mx(out=c_x2AB[:, 0:256].bitcast(FP8X4), scales=s_x2AB[:, 0:256], in_=g_x2AB[:, 0:1024])
+        nc.tensor.matmul_mx(out=acc[0][:], lhsT=c_w012[:, 256:384].bitcast(FP8X4), lhsT_scale=s_w012[:, 256:384], rhs=c_x2AB[:, 0:128].bitcast(FP8X4), rhs_scale=s_x2AB[:, 0:128], start=False, stop=True)
+        nc.tensor.matmul_mx(out=acc[1][:], lhsT=c_w012[:, 256:384].bitcast(FP8X4), lhsT_scale=s_w012[:, 256:384], rhs=c_x2AB[:, 128:256].bitcast(FP8X4), rhs_scale=s_x2AB[:, 128:256], start=False, stop=True)
+        nc.scalar.activation(out=y[:, 128:256], in_=acc[1][:], func=GELU, bias=bias[:])
+        nc.scalar.activation(out=y[:, 0:128], in_=acc[0][:], func=GELU, bias=bias[:])
+        nc.vector.tensor_copy(out=g_x0CD[:, 0:512].rearrange("p (c i j) -> p c j i", i=RUN, j=PACK), in_=r_x0CD[:, :, 0:128].rearrange("p j (c i) -> p c j i", i=RUN))
+        nc.vector.quantize_mx(out=c_x0CD[:, 0:128].bitcast(FP8X4), scales=s_x0CD[:, 0:128], in_=g_x0CD[:, 0:512])
+        nc.tensor.matmul_mx(out=acc[2][:], lhsT=c_w012[:, 0:128].bitcast(FP8X4), lhsT_scale=s_w012[:, 0:128], rhs=c_x0CD[:, 0:128].bitcast(FP8X4), rhs_scale=s_x0CD[:, 0:128], start=True, stop=False)
+        nc.scalar.copy(out=g_x1C[:, 0:512].rearrange("p (c i j) -> p c j i", i=RUN, j=PACK), in_=r_x1C[:, :, 0:128].rearrange("p j (c i) -> p c j i", i=RUN))
+        nc.vector.quantize_mx(out=c_x1C[:, 0:128].bitcast(FP8X4), scales=s_x1C[:, 0:128], in_=g_x1C[:, 0:512])
+        nc.tensor.matmul_mx(out=acc[2][:], lhsT=c_w012[:, 128:256].bitcast(FP8X4), lhsT_scale=s_w012[:, 128:256], rhs=c_x1C[:, 0:128].bitcast(FP8X4), rhs_scale=s_x1C[:, 0:128], start=False, stop=False)
+        nc.vector.tensor_tensor(window[:].indirect(offsets[:, 0:8]), y[:, 0:128], gates[:, 0:128], mybir.AluOpType.mult)
+        nc.vector.tensor_tensor(window[:].indirect(offsets[:, 8:16]), y[:, 128:256], gates[:, 128:256], mybir.AluOpType.mult)
+        nc.scalar.copy(out=g_x2C[:, 0:512].rearrange("p (c i j) -> p c j i", i=RUN, j=PACK), in_=r_x2C[:, :, 0:128].rearrange("p j (c i) -> p c j i", i=RUN))
+        nc.vector.quantize_mx(out=c_x2C[:, 0:128].bitcast(FP8X4), scales=s_x2C[:, 0:128], in_=g_x2C[:, 0:512])
+        nc.tensor.matmul_mx(out=acc[2][:], lhsT=c_w012[:, 256:384].bitcast(FP8X4), lhsT_scale=s_w012[:, 256:384], rhs=c_x2C[:, 0:128].bitcast(FP8X4), rhs_scale=s_x2C[:, 0:128], start=False, stop=True)
+        nc.vector.tensor_copy(out=g_x2D[:, 0:512].rearrange("p (c i j) -> p c j i", i=RUN, j=PACK), in_=r_x2D[:, :, 0:128].rearrange("p j (c i) -> p c j i", i=RUN))
+        nc.scalar.activation(out=y[:, 256:384], in_=acc[2][:], func=GELU, bias=bias[:])
+        nc.vector.quantize_mx(out=c_x2D[:, 0:128].bitcast(FP8X4), scales=s_x2D[:, 0:128], in_=g_x2D[:, 0:512])
+        nc.scalar.copy(out=g_x1D[:, 0:512].rearrange("p (c i j) -> p c j i", i=RUN, j=PACK), in_=r_x1D[:, :, 0:128].rearrange("p j (c i) -> p c j i", i=RUN))
+        nc.vector.quantize_mx(out=c_x1D[:, 0:128].bitcast(FP8X4), scales=s_x1D[:, 0:128], in_=g_x1D[:, 0:512])
+        nc.tensor.matmul_mx(out=acc[3][:], lhsT=c_w012[:, 128:256].bitcast(FP8X4), lhsT_scale=s_w012[:, 128:256], rhs=c_x1D[:, 0:128].bitcast(FP8X4), rhs_scale=s_x1D[:, 0:128], start=False, stop=False)
+        nc.tensor.matmul_mx(out=acc[3][:], lhsT=c_w012[:, 256:384].bitcast(FP8X4), lhsT_scale=s_w012[:, 256:384], rhs=c_x2D[:, 0:128].bitcast(FP8X4), rhs_scale=s_x2D[:, 0:128], start=False, stop=True)
+        nc.scalar.activation(out=y[:, 384:512], in_=acc[3][:], func=GELU, bias=bias[:])
+        nc.vector.tensor_tensor(window[:].indirect(offsets[:, 16:24]), y[:, 256:384], gates[:, 256:384], mybir.AluOpType.mult)
+        nc.vector.tensor_tensor(window[:].indirect(offsets[:, 24:32]), y[:, 384:512], gates[:, 384:512], mybir.AluOpType.mult)
         nc.sync.dma_start(out=out, in_=window[:])

@@ -42,103 +42,97 @@ def tile_picked_place_lin_gelu_sub_l_kernel(tc, xT, w, b, gate, offs, out):
         nc.scalar.activation(out=warm_out[:], in_=warm_in[:], func=GELU)
         nc.vector.memset(window[:], 0.0)
         gates = keep.tile([P, S], F32, name="gates")
-        r_w012 = keep.tile([P, 3, PACK, N], F32, name="r_w012")
-        nc.sync.dma_start(out=r_w012[:], in_=w[0:1536, :].rearrange("(c p j) n -> p c j n", p=P, j=PACK))
-        g_w012 = keep.tile([P, 1536], BF16, name="g_w012", align_bytes=64)
-        c_w012 = keep.tile([P, 384], U32, name="c_w012", align_bytes=64)
-        s_w012 = keep.tile([P, 384], U8, name="s_w012", align_bytes=64)
-        r_x0AB = keep.tile([P, PACK, 256], F32, name="r_x0AB")
-        nc.sync.dma_start(out=r_x0AB[:], in_=xT[0:512, 0:256].rearrange("(p j) n -> p j n", j=PACK))
-        g_x0AB = keep.tile([P, 1024], BF16, name="g_x0AB", align_bytes=64)
-        c_x0AB = keep.tile([P, 256], U32, name="c_x0AB", align_bytes=64)
-        s_x0AB = keep.tile([P, 256], U8, name="s_x0AB", align_bytes=64)
-        r_x1AB = keep.tile([P, PACK, 256], F32, name="r_x1AB")
-        nc.sync.dma_start(out=r_x1AB[:], in_=xT[512:1024, 0:256].rearrange("(p j) n -> p j n", j=PACK))
-        g_x1AB = keep.tile([P, 1024], BF16, name="g_x1AB", align_bytes=64)
-        c_x1AB = keep.tile([P, 256], U32, name="c_x1AB", align_bytes=64)
-        s_x1AB = keep.tile([P, 256], U8, name="s_x1AB", align_bytes=64)
-        r_x2AB = keep.tile([P, PACK, 256], F32, name="r_x2AB")
-        nc.sync.dma_start(out=r_x2AB[:], in_=xT[1024:1536, 0:256].rearrange("(p j) n -> p j n", j=PACK))
-        g_x2AB = keep.tile([P, 1024], BF16, name="g_x2AB", align_bytes=64)
-        c_x2AB = keep.tile([P, 256], U32, name="c_x2AB", align_bytes=64)
-        s_x2AB = keep.tile([P, 256], U8, name="s_x2AB", align_bytes=64)
-        r_x0CD = keep.tile([P, PACK, 256], F32, name="r_x0CD")
-        nc.sync.dma_start(out=r_x0CD[:], in_=xT[0:512, 256:512].rearrange("(p j) n -> p j n", j=PACK))
-        g_x0CD = keep.tile([P, 1024], BF16, name="g_x0CD", align_bytes=64)
-        c_x0CD = keep.tile([P, 256], U32, name="c_x0CD", align_bytes=64)
-        s_x0CD = keep.tile([P, 256], U8, name="s_x0CD", align_bytes=64)
+        r_x0ABCD = keep.tile([P, PACK, 512], F32, name="r_x0ABCD")
+        nc.sync.dma_start(out=r_x0ABCD[:], in_=xT[0:512, 0:512].rearrange("(p j) n -> p j n", j=PACK))
+        g_x0ABCD = keep.tile([P, 2048], BF16, name="g_x0ABCD", align_bytes=64)
+        c_x0ABCD = keep.tile([P, 512], U32, name="c_x0ABCD", align_bytes=64)
+        s_x0ABCD = keep.tile([P, 512], U8, name="s_x0ABCD", align_bytes=64)
+        r_x1ABCD = keep.tile([P, PACK, 512], F32, name="r_x1ABCD")
+        nc.sync.dma_start(out=r_x1ABCD[:], in_=xT[512:1024, 0:512].rearrange("(p j) n -> p j n", j=PACK))
+        g_x1ABCD = keep.tile([P, 2048], BF16, name="g_x1ABCD", align_bytes=64)
+        c_x1ABCD = keep.tile([P, 512], U32, name="c_x1ABCD", align_bytes=64)
+        s_x1ABCD = keep.tile([P, 512], U8, name="s_x1ABCD", align_bytes=64)
+        r_w0 = keep.tile([P, 1, PACK, N], F32, name="r_w0")
+        nc.sync.dma_start(out=r_w0[:], in_=w[0:512, :].rearrange("(c p j) n -> p c j n", p=P, j=PACK))
+        g_w0 = keep.tile([P, 512], BF16, name="g_w0", align_bytes=64)
+        c_w0 = keep.tile([P, 128], U32, name="c_w0", align_bytes=64)
+        s_w0 = keep.tile([P, 128], U8, name="s_w0", align_bytes=64)
+        r_w1 = keep.tile([P, 1, PACK, N], F32, name="r_w1")
+        nc.sync.dma_start(out=r_w1[:], in_=w[512:1024, :].rearrange("(c p j) n -> p c j n", p=P, j=PACK))
+        g_w1 = keep.tile([P, 512], BF16, name="g_w1", align_bytes=64)
+        c_w1 = keep.tile([P, 128], U32, name="c_w1", align_bytes=64)
+        s_w1 = keep.tile([P, 128], U8, name="s_w1", align_bytes=64)
+        r_w2 = keep.tile([P, 1, PACK, N], F32, name="r_w2")
+        nc.sync.dma_start(out=r_w2[:], in_=w[1024:1536, :].rearrange("(c p j) n -> p c j n", p=P, j=PACK))
+        g_w2 = keep.tile([P, 512], BF16, name="g_w2", align_bytes=64)
+        c_w2 = keep.tile([P, 128], U32, name="c_w2", align_bytes=64)
+        s_w2 = keep.tile([P, 128], U8, name="s_w2", align_bytes=64)
+        r_x2A = keep.tile([P, PACK, 128], F32, name="r_x2A")
+        nc.sync.dma_start(out=r_x2A[:], in_=xT[1024:1536, 0:128].rearrange("(p j) n -> p j n", j=PACK))
+        g_x2A = keep.tile([P, 512], BF16, name="g_x2A", align_bytes=64)
+        c_x2A = keep.tile([P, 128], U32, name="c_x2A", align_bytes=64)
+        s_x2A = keep.tile([P, 128], U8, name="s_x2A", align_bytes=64)
+        r_x2B = keep.tile([P, PACK, 128], F32, name="r_x2B")
+        nc.sync.dma_start(out=r_x2B[:], in_=xT[1024:1536, 128:256].rearrange("(p j) n -> p j n", j=PACK))
+        g_x2B = keep.tile([P, 512], BF16, name="g_x2B", align_bytes=64)
+        c_x2B = keep.tile([P, 128], U32, name="c_x2B", align_bytes=64)
+        s_x2B = keep.tile([P, 128], U8, name="s_x2B", align_bytes=64)
         nc.sync.dma_start(offsets[:], offs)
-        r_x1C = keep.tile([P, PACK, 128], F32, name="r_x1C")
-        nc.sync.dma_start(out=r_x1C[:], in_=xT[512:1024, 256:384].rearrange("(p j) n -> p j n", j=PACK))
-        g_x1C = keep.tile([P, 512], BF16, name="g_x1C", align_bytes=64)
-        c_x1C = keep.tile([P, 128], U32, name="c_x1C", align_bytes=64)
-        s_x1C = keep.tile([P, 128], U8, name="s_x1C", align_bytes=64)
-        nc.sync.dma_start(out=gates[:, 0:256], in_=gate[:, 0:256])
         r_x2C = keep.tile([P, PACK, 128], F32, name="r_x2C")
         nc.sync.dma_start(out=r_x2C[:], in_=xT[1024:1536, 256:384].rearrange("(p j) n -> p j n", j=PACK))
         g_x2C = keep.tile([P, 512], BF16, name="g_x2C", align_bytes=64)
         c_x2C = keep.tile([P, 128], U32, name="c_x2C", align_bytes=64)
         s_x2C = keep.tile([P, 128], U8, name="s_x2C", align_bytes=64)
-        r_x1D = keep.tile([P, PACK, 128], F32, name="r_x1D")
-        nc.sync.dma_start(out=r_x1D[:], in_=xT[512:1024, 384:512].rearrange("(p j) n -> p j n", j=PACK))
-        g_x1D = keep.tile([P, 512], BF16, name="g_x1D", align_bytes=64)
-        c_x1D = keep.tile([P, 128], U32, name="c_x1D", align_bytes=64)
-        s_x1D = keep.tile([P, 128], U8, name="s_x1D", align_bytes=64)
+        nc.sync.dma_start(out=gates[:, 0:128], in_=gate[:, 0:128])
         r_x2D = keep.tile([P, PACK, 128], F32, name="r_x2D")
         nc.sync.dma_start(out=r_x2D[:], in_=xT[1024:1536, 384:512].rearrange("(p j) n -> p j n", j=PACK))
         g_x2D = keep.tile([P, 512], BF16, name="g_x2D", align_bytes=64)
         c_x2D = keep.tile([P, 128], U32, name="c_x2D", align_bytes=64)
         s_x2D = keep.tile([P, 128], U8, name="s_x2D", align_bytes=64)
+        nc.sync.dma_start(out=gates[:, 128:256], in_=gate[:, 128:256])
         nc.sync.dma_start(out=gates[:, 256:512], in_=gate[:, 256:512])
         acc = [psum.tile([N, CHUNK], F32, name="acc%d" % i) for i in range(CHUNKS)]
         y = keep.tile([N, S], F32, name="y")
-        nc.vector.tensor_copy(out=g_w012[:, 0:512].rearrange("p (c i j) -> p c j i", i=RUN, j=PACK), in_=r_w012[:, 0, :, 0:128].rearrange("p j (c i) -> p c j i", i=RUN))
-        nc.vector.tensor_copy(out=g_w012[:, 512:1024].rearrange("p (c i j) -> p c j i", i=RUN, j=PACK), in_=r_w012[:, 1, :, 0:128].rearrange("p j (c i) -> p c j i", i=RUN))
-        nc.scalar.copy(out=g_x0AB[:, 512:1024].rearrange("p (c i j) -> p c j i", i=RUN, j=PACK), in_=r_x0AB[:, :, 128:256].rearrange("p j (c i) -> p c j i", i=RUN))
-        nc.vector.tensor_copy(out=g_x0AB[:, 0:512].rearrange("p (c i j) -> p c j i", i=RUN, j=PACK), in_=r_x0AB[:, :, 0:128].rearrange("p j (c i) -> p c j i", i=RUN))
-        nc.vector.quantize_mx(out=c_x0AB[:, 0:128].bitcast(FP8X4), scales=s_x0AB[:, 0:128], in_=g_x0AB[:, 0:512])
-        nc.vector.quantize_mx(out=c_w012[:, 0:128].bitcast(FP8X4), scales=s_w012[:, 0:128], in_=g_w012[:, 0:512])
-        nc.tensor.matmul_mx(out=acc[0][:], lhsT=c_w012[:, 0:128].bitcast(FP8X4), lhsT_scale=s_w012[:, 0:128], rhs=c_x0AB[:, 0:128].bitcast(FP8X4), rhs_scale=s_x0AB[:, 0:128], start=True, stop=False)
-        nc.vector.tensor_copy(out=g_x1AB[:, 512:1024].rearrange("p (c i j) -> p c j i", i=RUN, j=PACK), in_=r_x1AB[:, :, 128:256].rearrange("p j (c i) -> p c j i", i=RUN))
-        nc.vector.quantize_mx(out=c_x1AB[:, 128:256].bitcast(FP8X4), scales=s_x1AB[:, 128:256], in_=g_x1AB[:, 512:1024])
-        nc.scalar.copy(out=g_x2AB[:, 768:1024].rearrange("p (c i j) -> p c j i", i=RUN, j=PACK), in_=r_x2AB[:, :, 192:256].rearrange("p j (c i) -> p c j i", i=RUN))
-        nc.vector.tensor_copy(out=g_x2AB[:, 512:768].rearrange("p (c i j) -> p c j i", i=RUN, j=PACK), in_=r_x2AB[:, :, 128:192].rearrange("p j (c i) -> p c j i", i=RUN))
-        nc.vector.quantize_mx(out=c_x0AB[:, 128:256].bitcast(FP8X4), scales=s_x0AB[:, 128:256], in_=g_x0AB[:, 512:1024])
-        nc.tensor.matmul_mx(out=acc[1][:], lhsT=c_w012[:, 0:128].bitcast(FP8X4), lhsT_scale=s_w012[:, 0:128], rhs=c_x0AB[:, 128:256].bitcast(FP8X4), rhs_scale=s_x0AB[:, 128:256], start=True, stop=False)
-        nc.scalar.copy(out=g_w012[:, 1024:1536].rearrange("p (c i j) -> p c j i", i=RUN, j=PACK), in_=r_w012[:, 2, :, 0:128].rearrange("p j (c i) -> p c j i", i=RUN))
-        nc.vector.quantize_mx(out=c_w012[:, 128:384].bitcast(FP8X4), scales=s_w012[:, 128:384], in_=g_w012[:, 512:1536])
-        nc.tensor.matmul_mx(out=acc[1][:], lhsT=c_w012[:, 128:256].bitcast(FP8X4), lhsT_scale=s_w012[:, 128:256], rhs=c_x1AB[:, 128:256].bitcast(FP8X4), rhs_scale=s_x1AB[:, 128:256], start=False, stop=False)
-        nc.scalar.copy(out=g_x1AB[:, 0:512].rearrange("p (c i j) -> p c j i", i=RUN, j=PACK), in_=r_x1AB[:, :, 0:128].rearrange("p j (c i) -> p c j i", i=RUN))
-        nc.vector.quantize_mx(out=c_x1AB[:, 0:128].bitcast(FP8X4), scales=s_x1AB[:, 0:128], in_=g_x1AB[:, 0:512])
-        nc.tensor.matmul_mx(out=acc[0][:], lhsT=c_w012[:, 128:256].bitcast(FP8X4), lhsT_scale=s_w012[:, 128:256], rhs=c_x1AB[:, 0:128].bitcast(FP8X4), rhs_scale=s_x1AB[:, 0:128], start=False, stop=False)
-        nc.vector.tensor_copy(out=g_x2AB[:, 0:512].rearrange("p (c i j) -> p c j i", i=RUN, j=PACK), in_=r_x2AB[:, :, 0:128].rearrange("p j (c i) -> p c j i", i=RUN))
-        nc.vector.tensor_copy(out=g_x0CD[:, 512:1024].rearrange("p (c i j) -> p c j i", i=RUN, j=PACK), in_=r_x0CD[:, :, 128:256].rearrange("p j (c i) -> p c j i", i=RUN))
-        nc.vector.quantize_mx(out=c_x0CD[:, 128:256].bitcast(FP8X4), scales=s_x0CD[:, 128:256], in_=g_x0CD[:, 512:1024])
-        nc.tensor.matmul_mx(out=acc[3][:], lhsT=c_w012[:, 0:128].bitcast(FP8X4), lhsT_scale=s_w012[:, 0:128], rhs=c_x0CD[:, 128:256].bitcast(FP8X4), rhs_scale=s_x0CD[:, 128:256], start=True, stop=False)
-        nc.vector.quantize_mx(out=c_x2AB[:, 0:256].bitcast(FP8X4), scales=s_x2AB[:, 0:256], in_=g_x2AB[:, 0:1024])
-        nc.tensor.matmul_mx(out=acc[0][:], lhsT=c_w012[:, 256:384].bitcast(FP8X4), lhsT_scale=s_w012[:, 256:384], rhs=c_x2AB[:, 0:128].bitcast(FP8X4), rhs_scale=s_x2AB[:, 0:128], start=False, stop=True)
-        nc.tensor.matmul_mx(out=acc[1][:], lhsT=c_w012[:, 256:384].bitcast(FP8X4), lhsT_scale=s_w012[:, 256:384], rhs=c_x2AB[:, 128:256].bitcast(FP8X4), rhs_scale=s_x2AB[:, 128:256], start=False, stop=True)
-        nc.scalar.activation(out=y[:, 128:256], in_=acc[1][:], func=GELU, bias=bias[:])
+        nc.vector.tensor_copy(out=g_x0ABCD[:, 0:1024].rearrange("p (c i j) -> p c j i", i=RUN, j=PACK), in_=r_x0ABCD[:, :, 0:256].rearrange("p j (c i) -> p c j i", i=RUN))
+        nc.scalar.copy(out=g_x0ABCD[:, 1024:2048].rearrange("p (c i j) -> p c j i", i=RUN, j=PACK), in_=r_x0ABCD[:, :, 256:512].rearrange("p j (c i) -> p c j i", i=RUN))
+        nc.vector.quantize_mx(out=c_x0ABCD[:, 0:256].bitcast(FP8X4), scales=s_x0ABCD[:, 0:256], in_=g_x0ABCD[:, 0:1024])
+        nc.vector.quantize_mx(out=c_x0ABCD[:, 256:512].bitcast(FP8X4), scales=s_x0ABCD[:, 256:512], in_=g_x0ABCD[:, 1024:2048])
+        nc.vector.tensor_copy(out=g_x1ABCD[:, 0:1024].rearrange("p (c i j) -> p c j i", i=RUN, j=PACK), in_=r_x1ABCD[:, :, 0:256].rearrange("p j (c i) -> p c j i", i=RUN))
+        nc.scalar.copy(out=g_x1ABCD[:, 1024:2048].rearrange("p (c i j) -> p c j i", i=RUN, j=PACK), in_=r_x1ABCD[:, :, 256:512].rearrange("p j (c i) -> p c j i", i=RUN))
+        nc.vector.quantize_mx(out=c_x1ABCD[:, 0:256].bitcast(FP8X4), scales=s_x1ABCD[:, 0:256], in_=g_x1ABCD[:, 0:1024])
+        nc.vector.quantize_mx(out=c_x1ABCD[:, 256:512].bitcast(FP8X4), scales=s_x1ABCD[:, 256:512], in_=g_x1ABCD[:, 1024:2048])
+        nc.vector.tensor_copy(out=g_w0[:, 0:512].rearrange("p (c i j) -> p c j i", i=RUN, j=PACK), in_=r_w0[:, 0, :, 0:128].rearrange("p j (c i) -> p c j i", i=RUN))
+        nc.vector.quantize_mx(out=c_w0[:, 0:128].bitcast(FP8X4), scales=s_w0[:, 0:128], in_=g_w0[:, 0:512])
+        nc.tensor.matmul_mx(out=acc[0][:], lhsT=c_w0[:, 0:128].bitcast(FP8X4), lhsT_scale=s_w0[:, 0:128], rhs=c_x0ABCD[:, 0:128].bitcast(FP8X4), rhs_scale=s_x0ABCD[:, 0:128], start=True, stop=False)
+        nc.tensor.matmul_mx(out=acc[1][:], lhsT=c_w0[:, 0:128].bitcast(FP8X4), lhsT_scale=s_w0[:, 0:128], rhs=c_x0ABCD[:, 128:256].bitcast(FP8X4), rhs_scale=s_x0ABCD[:, 128:256], start=True, stop=False)
+        nc.tensor.matmul_mx(out=acc[2][:], lhsT=c_w0[:, 0:128].bitcast(FP8X4), lhsT_scale=s_w0[:, 0:128], rhs=c_x0ABCD[:, 256:384].bitcast(FP8X4), rhs_scale=s_x0ABCD[:, 256:384], start=True, stop=False)
+        nc.tensor.matmul_mx(out=acc[3][:], lhsT=c_w0[:, 0:128].bitcast(FP8X4), lhsT_scale=s_w0[:, 0:128], rhs=c_x0ABCD[:, 384:512].bitcast(FP8X4), rhs_scale=s_x0ABCD[:, 384:512], start=True, stop=False)
+        nc.scalar.copy(out=g_w1[:, 0:512].rearrange("p (c i j) -> p c j i", i=RUN, j=PACK), in_=r_w1[:, 0, :, 0:128].rearrange("p j (c i) -> p c j i", i=RUN))
+        nc.vector.quantize_mx(out=c_w1[:, 0:128].bitcast(FP8X4), scales=s_w1[:, 0:128], in_=g_w1[:, 0:512])
+        nc.tensor.matmul_mx(out=acc[0][:], lhsT=c_w1[:, 0:128].bitcast(FP8X4), lhsT_scale=s_w1[:, 0:128], rhs=c_x1ABCD[:, 0:128].bitcast(FP8X4), rhs_scale=s_x1ABCD[:, 0:128], start=False, stop=False)
+        nc.tensor.matmul_mx(out=acc[1][:], lhsT=c_w1[:, 0:128].bitcast(FP8X4), lhsT_scale=s_w1[:, 0:128], rhs=c_x1ABCD[:, 128:256].bitcast(FP8X4), rhs_scale=s_x1ABCD[:, 128:256], start=False, stop=False)
+        nc.tensor.matmul_mx(out=acc[2][:], lhsT=c_w1[:, 0:128].bitcast(FP8X4), lhsT_scale=s_w1[:, 0:128], rhs=c_x1ABCD[:, 256:384].bitcast(FP8X4), rhs_scale=s_x1ABCD[:, 256:384], start=False, stop=False)
+        nc.tensor.matmul_mx(out=acc[3][:], lhsT=c_w1[:, 0:128].bitcast(FP8X4), lhsT_scale=s_w1[:, 0:128], rhs=c_x1ABCD[:, 384:512].bitcast(FP8X4), rhs_scale=s_x1ABCD[:, 384:512], start=False, stop=False)
+        nc.scalar.copy(out=g_w2[:, 0:512].rearrange("p (c i j) -> p c j i", i=RUN, j=PACK), in_=r_w2[:, 0, :, 0:128].rearrange("p j (c i) -> p c j i", i=RUN))
+        nc.vector.quantize_mx(out=c_w2[:, 0:128].bitcast(FP8X4), scales=s_w2[:, 0:128], in_=g_w2[:, 0:512])
+        nc.vector.tensor_copy(out=g_x2A[:, 0:512].rearrange("p (c i j) -> p c j i", i=RUN, j=PACK), in_=r_x2A[:, :, 0:128].rearrange("p j (c i) -> p c j i", i=RUN))
+        nc.vector.quantize_mx(out=c_x2A[:, 0:128].bitcast(FP8X4), scales=s_x2A[:, 0:128], in_=g_x2A[:, 0:512])
+        nc.tensor.matmul_mx(out=acc[0][:], lhsT=c_w2[:, 0:128].bitcast(FP8X4), lhsT_scale=s_w2[:, 0:128], rhs=c_x2A[:, 0:128].bitcast(FP8X4), rhs_scale=s_x2A[:, 0:128], start=False, stop=True)
+        nc.scalar.copy(out=g_x2B[:, 0:512].rearrange("p (c i j) -> p c j i", i=RUN, j=PACK), in_=r_x2B[:, :, 0:128].rearrange("p j (c i) -> p c j i", i=RUN))
+        nc.vector.quantize_mx(out=c_x2B[:, 0:128].bitcast(FP8X4), scales=s_x2B[:, 0:128], in_=g_x2B[:, 0:512])
+        nc.tensor.matmul_mx(out=acc[1][:], lhsT=c_w2[:, 0:128].bitcast(FP8X4), lhsT_scale=s_w2[:, 0:128], rhs=c_x2B[:, 0:128].bitcast(FP8X4), rhs_scale=s_x2B[:, 0:128], start=False, stop=True)
         nc.scalar.activation(out=y[:, 0:128], in_=acc[0][:], func=GELU, bias=bias[:])
-        nc.vector.tensor_copy(out=g_x0CD[:, 0:512].rearrange("p (c i j) -> p c j i", i=RUN, j=PACK), in_=r_x0CD[:, :, 0:128].rearrange("p j (c i) -> p c j i", i=RUN))
-        nc.vector.quantize_mx(out=c_x0CD[:, 0:128].bitcast(FP8X4), scales=s_x0CD[:, 0:128], in_=g_x0CD[:, 0:512])
-        nc.tensor.matmul_mx(out=acc[2][:], lhsT=c_w012[:, 0:128].bitcast(FP8X4), lhsT_scale=s_w012[:, 0:128], rhs=c_x0CD[:, 0:128].bitcast(FP8X4), rhs_scale=s_x0CD[:, 0:128], start=True, stop=False)
-        nc.scalar.copy(out=g_x1C[:, 0:512].rearrange("p (c i j) -> p c j i", i=RUN, j=PACK), in_=r_x1C[:, :, 0:128].rearrange("p j (c i) -> p c j i", i=RUN))
-        nc.vector.quantize_mx(out=c_x1C[:, 0:128].bitcast(FP8X4), scales=s_x1C[:, 0:128], in_=g_x1C[:, 0:512])
-        nc.tensor.matmul_mx(out=acc[2][:], lhsT=c_w012[:, 128:256].bitcast(FP8X4), lhsT_scale=s_w012[:, 128:256], rhs=c_x1C[:, 0:128].bitcast(FP8X4), rhs_scale=s_x1C[:, 0:128], start=False, stop=False)
-        nc.vector.tensor_tensor(window[:].indirect(offsets[:, 0:8]), y[:, 0:128], gates[:, 0:128], mybir.AluOpType.mult)
-        nc.vector.tensor_tensor(window[:].indirect(offsets[:, 8:16]), y[:, 128:256], gates[:, 128:256], mybir.AluOpType.mult)
         nc.scalar.copy(out=g_x2C[:, 0:512].rearrange("p (c i j) -> p c j i", i=RUN, j=PACK), in_=r_x2C[:, :, 0:128].rearrange("p j (c i) -> p c j i", i=RUN))
         nc.vector.quantize_mx(out=c_x2C[:, 0:128].bitcast(FP8X4), scales=s_x2C[:, 0:128], in_=g_x2C[:, 0:512])
-        nc.tensor.matmul_mx(out=acc[2][:], lhsT=c_w012[:, 256:384].bitcast(FP8X4), lhsT_scale=s_w012[:, 256:384], rhs=c_x2C[:, 0:128].bitcast(FP8X4), rhs_scale=s_x2C[:, 0:128], start=False, stop=True)
-        nc.vector.tensor_copy(out=g_x2D[:, 0:512].rearrange("p (c i j) -> p c j i", i=RUN, j=PACK), in_=r_x2D[:, :, 0:128].rearrange("p j (c i) -> p c j i", i=RUN))
-        nc.scalar.activation(out=y[:, 256:384], in_=acc[2][:], func=GELU, bias=bias[:])
+        nc.tensor.matmul_mx(out=acc[2][:], lhsT=c_w2[:, 0:128].bitcast(FP8X4), lhsT_scale=s_w2[:, 0:128], rhs=c_x2C[:, 0:128].bitcast(FP8X4), rhs_scale=s_x2C[:, 0:128], start=False, stop=True)
+        nc.scalar.activation(out=r_x2C[:, 0, 0:128], in_=acc[1][:], func=GELU, bias=bias[:])
+        nc.scalar.copy(out=g_x2D[:, 0:512].rearrange("p (c i j) -> p c j i", i=RUN, j=PACK), in_=r_x2D[:, :, 0:128].rearrange("p j (c i) -> p c j i", i=RUN))
         nc.vector.quantize_mx(out=c_x2D[:, 0:128].bitcast(FP8X4), scales=s_x2D[:, 0:128], in_=g_x2D[:, 0:512])
-        nc.scalar.copy(out=g_x1D[:, 0:512].rearrange("p (c i j) -> p c j i", i=RUN, j=PACK), in_=r_x1D[:, :, 0:128].rearrange("p j (c i) -> p c j i", i=RUN))
-        nc.vector.quantize_mx(out=c_x1D[:, 0:128].bitcast(FP8X4), scales=s_x1D[:, 0:128], in_=g_x1D[:, 0:512])
-        nc.tensor.matmul_mx(out=acc[3][:], lhsT=c_w012[:, 128:256].bitcast(FP8X4), lhsT_scale=s_w012[:, 128:256], rhs=c_x1D[:, 0:128].bitcast(FP8X4), rhs_scale=s_x1D[:, 0:128], start=False, stop=False)
-        nc.tensor.matmul_mx(out=acc[3][:], lhsT=c_w012[:, 256:384].bitcast(FP8X4), lhsT_scale=s_w012[:, 256:384], rhs=c_x2D[:, 0:128].bitcast(FP8X4), rhs_scale=s_x2D[:, 0:128], start=False, stop=True)
+        nc.tensor.matmul_mx(out=acc[3][:], lhsT=c_w2[:, 0:128].bitcast(FP8X4), lhsT_scale=s_w2[:, 0:128], rhs=c_x2D[:, 0:128].bitcast(FP8X4), rhs_scale=s_x2D[:, 0:128], start=False, stop=True)
         nc.scalar.activation(out=y[:, 384:512], in_=acc[3][:], func=GELU, bias=bias[:])
-        nc.vector.tensor_tensor(window[:].indirect(offsets[:, 16:24]), y[:, 256:384], gates[:, 256:384], mybir.AluOpType.mult)
+        nc.vector.tensor_tensor(window[:].indirect(offsets[:, 0:8]), y[:, 0:128], gates[:, 0:128], mybir.AluOpType.mult)
+        nc.scalar.activation(out=r_x2D[:, 0, 0:128], in_=acc[2][:], func=GELU, bias=bias[:])
+        nc.vector.tensor_tensor(window[:].indirect(offsets[:, 8:16]), r_x2C[:, 0, 0:128], gates[:, 128:256], mybir.AluOpType.mult)
+        nc.vector.tensor_tensor(window[:].indirect(offsets[:, 16:24]), r_x2D[:, 0, 0:128], gates[:, 256:384], mybir.AluOpType.mult)
         nc.vector.tensor_tensor(window[:].indirect(offsets[:, 24:32]), y[:, 384:512], gates[:, 384:512], mybir.AluOpType.mult)
         nc.sync.dma_start(out=out, in_=window[:])

from contextlib import ExitStack

import concourse.mybir as mybir

K, T, S, N = 1536, 1024, 512, 128
FLOPS = 2 * K * S * N

F32 = mybir.dt.float32
BF16 = mybir.dt.bfloat16
U32 = mybir.dt.uint32
U16 = mybir.dt.uint16
U8 = mybir.dt.uint8
FP8X4 = mybir.dt.float8_e4m3fn_x4
GELU = mybir.ActivationFunctionType.Gelu_apprx_tanh

P = 128
PACK = 4
K_PASS = P * PACK
PASSES = K // K_PASS
CHUNK = 128
CHUNKS = S // CHUNK
LANES = 16
RUN = 4


def tile_picked_place_lin_gelu_sub_l_kernel(tc, xT, w, b, gate, offs, out):
    nc = tc.nc
    last = PASSES - 1

    with ExitStack() as ctx:
        keep = ctx.enter_context(tc.tile_pool(name="keep", bufs=1))
        psum = ctx.enter_context(tc.psum_pool(name="psum", bufs=1))

        offsets = keep.tile([P, S // LANES], U16, name="offsets")
        bias = keep.tile([P, 1], F32, name="bias")
        window = keep.tile([P, T], F32, name="window")
        warm_in = keep.tile([P, 1], F32, name="warm_in")
        warm_out = keep.tile([P, 1], F32, name="warm_out")

        nc.scalar.dma_start(out=bias[:], in_=b)
        nc.vector.memset(warm_in[:], 0.0)
        nc.scalar.activation(out=warm_out[:], in_=warm_in[:], func=GELU)
        nc.vector.memset(window[:], 0.0)
        gates = keep.tile([P, S], F32, name="gates")
        r_x0ABCD = keep.tile([P, PACK, 512], F32, name="r_x0ABCD")
        nc.sync.dma_start(out=r_x0ABCD[:], in_=xT[0:512, 0:512].rearrange("(p j) n -> p j n", j=PACK))
        g_x0ABCD = keep.tile([P, 2048], BF16, name="g_x0ABCD", align_bytes=64)
        c_x0ABCD = keep.tile([P, 512], U32, name="c_x0ABCD", align_bytes=64)
        s_x0ABCD = keep.tile([P, 512], U8, name="s_x0ABCD", align_bytes=64)
        r_x1ABCD = keep.tile([P, PACK, 512], F32, name="r_x1ABCD")
        nc.sync.dma_start(out=r_x1ABCD[:], in_=xT[512:1024, 0:512].rearrange("(p j) n -> p j n", j=PACK))
        g_x1ABCD = keep.tile([P, 2048], BF16, name="g_x1ABCD", align_bytes=64)
        c_x1ABCD = keep.tile([P, 512], U32, name="c_x1ABCD", align_bytes=64)
        s_x1ABCD = keep.tile([P, 512], U8, name="s_x1ABCD", align_bytes=64)
        r_w0 = keep.tile([P, 1, PACK, N], F32, name="r_w0")
        nc.sync.dma_start(out=r_w0[:], in_=w[0:512, :].rearrange("(c p j) n -> p c j n", p=P, j=PACK))
        g_w0 = keep.tile([P, 512], BF16, name="g_w0", align_bytes=64)
        c_w0 = keep.tile([P, 128], U32, name="c_w0", align_bytes=64)
        s_w0 = keep.tile([P, 128], U8, name="s_w0", align_bytes=64)
        r_w1 = keep.tile([P, 1, PACK, N], F32, name="r_w1")
        nc.sync.dma_start(out=r_w1[:], in_=w[512:1024, :].rearrange("(c p j) n -> p c j n", p=P, j=PACK))
        g_w1 = keep.tile([P, 512], BF16, name="g_w1", align_bytes=64)
        c_w1 = keep.tile([P, 128], U32, name="c_w1", align_bytes=64)
        s_w1 = keep.tile([P, 128], U8, name="s_w1", align_bytes=64)
        r_w2 = keep.tile([P, 1, PACK, N], F32, name="r_w2")
        nc.sync.dma_start(out=r_w2[:], in_=w[1024:1536, :].rearrange("(c p j) n -> p c j n", p=P, j=PACK))
        g_w2 = keep.tile([P, 512], BF16, name="g_w2", align_bytes=64)
        c_w2 = keep.tile([P, 128], U32, name="c_w2", align_bytes=64)
        s_w2 = keep.tile([P, 128], U8, name="s_w2", align_bytes=64)
        r_x2A = keep.tile([P, PACK, 128], F32, name="r_x2A")
        nc.sync.dma_start(out=r_x2A[:], in_=xT[1024:1536, 0:128].rearrange("(p j) n -> p j n", j=PACK))
        g_x2A = keep.tile([P, 512], BF16, name="g_x2A", align_bytes=64)
        c_x2A = keep.tile([P, 128], U32, name="c_x2A", align_bytes=64)
        s_x2A = keep.tile([P, 128], U8, name="s_x2A", align_bytes=64)
        r_x2B = keep.tile([P, PACK, 128], F32, name="r_x2B")
        nc.sync.dma_start(out=r_x2B[:], in_=xT[1024:1536, 128:256].rearrange("(p j) n -> p j n", j=PACK))
        g_x2B = keep.tile([P, 512], BF16, name="g_x2B", align_bytes=64)
        c_x2B = keep.tile([P, 128], U32, name="c_x2B", align_bytes=64)
        s_x2B = keep.tile([P, 128], U8, name="s_x2B", align_bytes=64)
        nc.sync.dma_start(offsets[:], offs)
        r_x2C = keep.tile([P, PACK, 128], F32, name="r_x2C")
        nc.sync.dma_start(out=r_x2C[:], in_=xT[1024:1536, 256:384].rearrange("(p j) n -> p j n", j=PACK))
        g_x2C = keep.tile([P, 512], BF16, name="g_x2C", align_bytes=64)
        c_x2C = keep.tile([P, 128], U32, name="c_x2C", align_bytes=64)
        s_x2C = keep.tile([P, 128], U8, name="s_x2C", align_bytes=64)
        nc.sync.dma_start(out=gates[:, 0:128], in_=gate[:, 0:128])
        r_x2D = keep.tile([P, PACK, 128], F32, name="r_x2D")
        nc.sync.dma_start(out=r_x2D[:], in_=xT[1024:1536, 384:512].rearrange("(p j) n -> p j n", j=PACK))
        g_x2D = keep.tile([P, 512], BF16, name="g_x2D", align_bytes=64)
        c_x2D = keep.tile([P, 128], U32, name="c_x2D", align_bytes=64)
        s_x2D = keep.tile([P, 128], U8, name="s_x2D", align_bytes=64)
        nc.sync.dma_start(out=gates[:, 128:256], in_=gate[:, 128:256])
        nc.sync.dma_start(out=gates[:, 256:512], in_=gate[:, 256:512])
        acc = [psum.tile([N, CHUNK], F32, name="acc%d" % i) for i in range(CHUNKS)]
        y = keep.tile([N, S], F32, name="y")
        nc.vector.tensor_copy(out=g_x0ABCD[:, 0:1024].rearrange("p (c i j) -> p c j i", i=RUN, j=PACK), in_=r_x0ABCD[:, :, 0:256].rearrange("p j (c i) -> p c j i", i=RUN))
        nc.scalar.copy(out=g_x0ABCD[:, 1024:2048].rearrange("p (c i j) -> p c j i", i=RUN, j=PACK), in_=r_x0ABCD[:, :, 256:512].rearrange("p j (c i) -> p c j i", i=RUN))
        nc.vector.quantize_mx(out=c_x0ABCD[:, 0:256].bitcast(FP8X4), scales=s_x0ABCD[:, 0:256], in_=g_x0ABCD[:, 0:1024])
        nc.vector.quantize_mx(out=c_x0ABCD[:, 256:512].bitcast(FP8X4), scales=s_x0ABCD[:, 256:512], in_=g_x0ABCD[:, 1024:2048])
        nc.vector.tensor_copy(out=g_x1ABCD[:, 0:1024].rearrange("p (c i j) -> p c j i", i=RUN, j=PACK), in_=r_x1ABCD[:, :, 0:256].rearrange("p j (c i) -> p c j i", i=RUN))
        nc.scalar.copy(out=g_x1ABCD[:, 1024:2048].rearrange("p (c i j) -> p c j i", i=RUN, j=PACK), in_=r_x1ABCD[:, :, 256:512].rearrange("p j (c i) -> p c j i", i=RUN))
        nc.vector.quantize_mx(out=c_x1ABCD[:, 0:256].bitcast(FP8X4), scales=s_x1ABCD[:, 0:256], in_=g_x1ABCD[:, 0:1024])
        nc.vector.quantize_mx(out=c_x1ABCD[:, 256:512].bitcast(FP8X4), scales=s_x1ABCD[:, 256:512], in_=g_x1ABCD[:, 1024:2048])
        nc.vector.tensor_copy(out=g_w0[:, 0:512].rearrange("p (c i j) -> p c j i", i=RUN, j=PACK), in_=r_w0[:, 0, :, 0:128].rearrange("p j (c i) -> p c j i", i=RUN))
        nc.vector.quantize_mx(out=c_w0[:, 0:128].bitcast(FP8X4), scales=s_w0[:, 0:128], in_=g_w0[:, 0:512])
        nc.tensor.matmul_mx(out=acc[0][:], lhsT=c_w0[:, 0:128].bitcast(FP8X4), lhsT_scale=s_w0[:, 0:128], rhs=c_x0ABCD[:, 0:128].bitcast(FP8X4), rhs_scale=s_x0ABCD[:, 0:128], start=True, stop=False)
        nc.tensor.matmul_mx(out=acc[1][:], lhsT=c_w0[:, 0:128].bitcast(FP8X4), lhsT_scale=s_w0[:, 0:128], rhs=c_x0ABCD[:, 128:256].bitcast(FP8X4), rhs_scale=s_x0ABCD[:, 128:256], start=True, stop=False)
        nc.tensor.matmul_mx(out=acc[2][:], lhsT=c_w0[:, 0:128].bitcast(FP8X4), lhsT_scale=s_w0[:, 0:128], rhs=c_x0ABCD[:, 256:384].bitcast(FP8X4), rhs_scale=s_x0ABCD[:, 256:384], start=True, stop=False)
        nc.tensor.matmul_mx(out=acc[3][:], lhsT=c_w0[:, 0:128].bitcast(FP8X4), lhsT_scale=s_w0[:, 0:128], rhs=c_x0ABCD[:, 384:512].bitcast(FP8X4), rhs_scale=s_x0ABCD[:, 384:512], start=True, stop=False)
        nc.scalar.copy(out=g_w1[:, 0:512].rearrange("p (c i j) -> p c j i", i=RUN, j=PACK), in_=r_w1[:, 0, :, 0:128].rearrange("p j (c i) -> p c j i", i=RUN))
        nc.vector.quantize_mx(out=c_w1[:, 0:128].bitcast(FP8X4), scales=s_w1[:, 0:128], in_=g_w1[:, 0:512])
        nc.tensor.matmul_mx(out=acc[0][:], lhsT=c_w1[:, 0:128].bitcast(FP8X4), lhsT_scale=s_w1[:, 0:128], rhs=c_x1ABCD[:, 0:128].bitcast(FP8X4), rhs_scale=s_x1ABCD[:, 0:128], start=False, stop=False)
        nc.tensor.matmul_mx(out=acc[1][:], lhsT=c_w1[:, 0:128].bitcast(FP8X4), lhsT_scale=s_w1[:, 0:128], rhs=c_x1ABCD[:, 128:256].bitcast(FP8X4), rhs_scale=s_x1ABCD[:, 128:256], start=False, stop=False)
        nc.tensor.matmul_mx(out=acc[2][:], lhsT=c_w1[:, 0:128].bitcast(FP8X4), lhsT_scale=s_w1[:, 0:128], rhs=c_x1ABCD[:, 256:384].bitcast(FP8X4), rhs_scale=s_x1ABCD[:, 256:384], start=False, stop=False)
        nc.tensor.matmul_mx(out=acc[3][:], lhsT=c_w1[:, 0:128].bitcast(FP8X4), lhsT_scale=s_w1[:, 0:128], rhs=c_x1ABCD[:, 384:512].bitcast(FP8X4), rhs_scale=s_x1ABCD[:, 384:512], start=False, stop=False)
        nc.scalar.copy(out=g_w2[:, 0:512].rearrange("p (c i j) -> p c j i", i=RUN, j=PACK), in_=r_w2[:, 0, :, 0:128].rearrange("p j (c i) -> p c j i", i=RUN))
        nc.vector.quantize_mx(out=c_w2[:, 0:128].bitcast(FP8X4), scales=s_w2[:, 0:128], in_=g_w2[:, 0:512])
        nc.vector.tensor_copy(out=g_x2A[:, 0:512].rearrange("p (c i j) -> p c j i", i=RUN, j=PACK), in_=r_x2A[:, :, 0:128].rearrange("p j (c i) -> p c j i", i=RUN))
        nc.vector.quantize_mx(out=c_x2A[:, 0:128].bitcast(FP8X4), scales=s_x2A[:, 0:128], in_=g_x2A[:, 0:512])
        nc.tensor.matmul_mx(out=acc[0][:], lhsT=c_w2[:, 0:128].bitcast(FP8X4), lhsT_scale=s_w2[:, 0:128], rhs=c_x2A[:, 0:128].bitcast(FP8X4), rhs_scale=s_x2A[:, 0:128], start=False, stop=True)
        nc.scalar.copy(out=g_x2B[:, 0:512].rearrange("p (c i j) -> p c j i", i=RUN, j=PACK), in_=r_x2B[:, :, 0:128].rearrange("p j (c i) -> p c j i", i=RUN))
        nc.vector.quantize_mx(out=c_x2B[:, 0:128].bitcast(FP8X4), scales=s_x2B[:, 0:128], in_=g_x2B[:, 0:512])
        nc.tensor.matmul_mx(out=acc[1][:], lhsT=c_w2[:, 0:128].bitcast(FP8X4), lhsT_scale=s_w2[:, 0:128], rhs=c_x2B[:, 0:128].bitcast(FP8X4), rhs_scale=s_x2B[:, 0:128], start=False, stop=True)
        nc.scalar.activation(out=y[:, 0:128], in_=acc[0][:], func=GELU, bias=bias[:])
        nc.scalar.copy(out=g_x2C[:, 0:512].rearrange("p (c i j) -> p c j i", i=RUN, j=PACK), in_=r_x2C[:, :, 0:128].rearrange("p j (c i) -> p c j i", i=RUN))
        nc.vector.quantize_mx(out=c_x2C[:, 0:128].bitcast(FP8X4), scales=s_x2C[:, 0:128], in_=g_x2C[:, 0:512])
        nc.tensor.matmul_mx(out=acc[2][:], lhsT=c_w2[:, 0:128].bitcast(FP8X4), lhsT_scale=s_w2[:, 0:128], rhs=c_x2C[:, 0:128].bitcast(FP8X4), rhs_scale=s_x2C[:, 0:128], start=False, stop=True)
        nc.scalar.activation(out=r_x2C[:, 0, 0:128], in_=acc[1][:], func=GELU, bias=bias[:])
        nc.scalar.copy(out=g_x2D[:, 0:512].rearrange("p (c i j) -> p c j i", i=RUN, j=PACK), in_=r_x2D[:, :, 0:128].rearrange("p j (c i) -> p c j i", i=RUN))
        nc.vector.quantize_mx(out=c_x2D[:, 0:128].bitcast(FP8X4), scales=s_x2D[:, 0:128], in_=g_x2D[:, 0:512])
        nc.tensor.matmul_mx(out=acc[3][:], lhsT=c_w2[:, 0:128].bitcast(FP8X4), lhsT_scale=s_w2[:, 0:128], rhs=c_x2D[:, 0:128].bitcast(FP8X4), rhs_scale=s_x2D[:, 0:128], start=False, stop=True)
        nc.scalar.activation(out=y[:, 384:512], in_=acc[3][:], func=GELU, bias=bias[:])
        nc.vector.tensor_tensor(window[:].indirect(offsets[:, 0:8]), y[:, 0:128], gates[:, 0:128], mybir.AluOpType.mult)
        nc.scalar.activation(out=r_x2D[:, 0, 0:128], in_=acc[2][:], func=GELU, bias=bias[:])
        nc.vector.tensor_tensor(window[:].indirect(offsets[:, 8:16]), r_x2C[:, 0, 0:128], gates[:, 128:256], mybir.AluOpType.mult)
        nc.vector.tensor_tensor(window[:].indirect(offsets[:, 16:24]), r_x2D[:, 0, 0:128], gates[:, 256:384], mybir.AluOpType.mult)
        nc.vector.tensor_tensor(window[:].indirect(offsets[:, 24:32]), y[:, 384:512], gates[:, 384:512], mybir.AluOpType.mult)
        nc.sync.dma_start(out=out, in_=window[:])
